import numpy as np
import ml_dtypes

BF16 = ml_dtypes.bfloat16


def bf(x):
    return np.asarray(x, np.float32).astype(BF16)


def f32(x):
    return np.asarray(x, np.float32)


def f64(x):
    return np.asarray(x).astype(np.float64)


def striped(idx):
    return np.tile(idx.reshape(-1, 16).T, (8, 1))


def rows(idx, k):
    return np.tile(idx, (k, 1))


def look(tab, idx):
    return np.take_along_axis(f64(tab), rows(idx, len(tab)), axis=1)


K, S, V, N, M = 512, 2048, 2048, 2048, 256


def setup_inputs():
    return {"tab": bf(np.random.standard_normal((2, K, S))), "x0": bf(np.random.standard_normal((K, V))), "w": bf(np.random.standard_normal((K, M)) / np.sqrt(K)), "b": f32(0.5 * np.random.standard_normal((M, 1))), "offs": striped(np.random.randint(0, S, N))}


def reference(tab, x0, w, b, offs):
    idx = offs[:16].T.reshape(-1)
    x = f64(x0) * look(tab[0], idx) + look(tab[1], idx)
    y = f64(w).T @ x
    return np.maximum(y + f64(b), 0.0)

@@ -1,0 +1,87 @@
+import concourse.mybir as mybir
+
+BF16, F32, U16 = mybir.dt.bfloat16, mybir.dt.float32, mybir.dt.uint16
+ADD, MULT = mybir.AluOpType.add, mybir.AluOpType.mult
+RELU = mybir.ActivationFunctionType.Relu
+
+P = 128
+R, S, N, M = 512, 2048, 2048, 256
+BLOCKS = R // P
+HALVES = M // P
+PIECE = 512
+PIECES = N // PIECE
+OFFSETS_PER_COLUMN = 16
+
+FLOPS = 2 * R * N * M + 2 * R * N
+
+
+def tile_lookup_film_mul_relu_kernel(tc, tab, x0, w, b, offs, out):
+    nc = tc.nc
+    with (
+        tc.tile_pool(name="held", bufs=1) as held,
+        tc.tile_pool(name="loaded", bufs=2) as loaded,
+        tc.tile_pool(name="wide", bufs=2) as wide,
+        tc.tile_pool(name="pieces", bufs=4) as pieces,
+        tc.psum_pool(name="psum", bufs=1) as psum,
+    ):
+        offsets = held.tile([P, N // OFFSETS_PER_COLUMN], U16)
+        nc.sync.dma_start(offsets[:], offs)
+
+        weights = held.tile([P, BLOCKS, M], BF16)
+        bias = held.tile([P, HALVES], F32)
+
+        sums = [
+            [psum.tile([P, PIECE], F32, name=f"sum_{h}_{c}") for c in range(PIECES)]
+            for h in range(HALVES)
+        ]
+
+        for r in range(BLOCKS):
+            rows = slice(r * P, (r + 1) * P)
+
+            gains_bf = loaded.tile([P, S], BF16)
+            nc.sync.dma_start(gains_bf[:], tab[0, rows, :])
+            features_bf = loaded.tile([P, N], BF16)
+            nc.sync.dma_start(features_bf[:], x0[rows, :])
+            shifts_bf = loaded.tile([P, S], BF16)
+            nc.sync.dma_start(shifts_bf[:], tab[1, rows, :])
+
+            if r == 0:
+                nc.sync.dma_start(weights[:], w.rearrange("(r p) m -> p r m", p=P))
+                nc.sync.dma_start(bias[:], b.rearrange("(h p) one -> p (h one)", p=P))
+
+            gains = wide.tile([P, S], F32)
+            nc.scalar.copy(gains[:], gains_bf[:])
+            features = wide.tile([P, N], F32)
+            nc.scalar.copy(features[:], features_bf[:])
+            shifts = wide.tile([P, S], F32)
+            nc.scalar.copy(shifts[:], shifts_bf[:])
+
+            scaled = wide.tile([P, N], F32)
+            nc.vector.tensor_tensor(scaled[:], gains[:].indirect(offsets[:]), features[:], MULT)
+
+            for c in range(PIECES):
+                columns = slice(c * PIECE, (c + 1) * PIECE)
+                list_columns = slice(
+                    c * PIECE // OFFSETS_PER_COLUMN, (c + 1) * PIECE // OFFSETS_PER_COLUMN
+                )
+                x = pieces.tile([P, PIECE], F32)
+                nc.vector.tensor_tensor(
+                    x[:], shifts[:].indirect(offsets[:, list_columns]), scaled[:, columns], ADD
+                )
+                x_bf = pieces.tile([P, PIECE], BF16)
+                nc.scalar.copy(x_bf[:], x[:])
+                for h in range(HALVES):
+                    nc.tensor.matmul(
+                        sums[h][c][:],
+                        weights[:, r, h * P : (h + 1) * P],
+                        x_bf[:],
+                        start=(r == 0),
+                        stop=(r == BLOCKS - 1),
+                    )
+
+        for c in range(PIECES):
+            columns = slice(c * PIECE, (c + 1) * PIECE)
+            for h in range(HALVES):
+                result = pieces.tile([P, PIECE], F32)
+                nc.scalar.activation(result[:], sums[h][c][:], RELU, bias=bias[:, h : h + 1])
+                nc.sync.dma_start(out[h * P : (h + 1) * P, columns], result[:])

@@ -1,7 +1,7 @@
 import concourse.mybir as mybir
 
 BF16, F32, U16 = mybir.dt.bfloat16, mybir.dt.float32, mybir.dt.uint16
-ADD, MULT = mybir.AluOpType.add, mybir.AluOpType.mult
+ADD, MAX, MULT = mybir.AluOpType.add, mybir.AluOpType.max, mybir.AluOpType.mult
 RELU = mybir.ActivationFunctionType.Relu
 
 P = 128
@@ -13,6 +13,15 @@ PIECES = N // PIECE
 OFFSETS_PER_COLUMN = 16
 
 FLOPS = 2 * R * N * M + 2 * R * N
+
+
+def columns(c):
+    return slice(c * PIECE, (c + 1) * PIECE)
+
+
+def list_columns(c):
+    width = PIECE // OFFSETS_PER_COLUMN
+    return slice(c * width, (c + 1) * width)
 
 
 def tile_lookup_film_mul_relu_kernel(tc, tab, x0, w, b, offs, out):
@@ -35,53 +44,74 @@ def tile_lookup_film_mul_relu_kernel(tc, tab, x0, w, b, offs, out):
             for h in range(HALVES)
         ]
 
-        for r in range(BLOCKS):
+        def load_and_widen(r):
             rows = slice(r * P, (r + 1) * P)
-
-            gains_bf = loaded.tile([P, S], BF16)
-            nc.sync.dma_start(gains_bf[:], tab[0, rows, :])
             features_bf = loaded.tile([P, N], BF16)
             nc.sync.dma_start(features_bf[:], x0[rows, :])
+            gains_bf = loaded.tile([P, S], BF16)
+            nc.sync.dma_start(gains_bf[:], tab[0, rows, :])
             shifts_bf = loaded.tile([P, S], BF16)
             nc.sync.dma_start(shifts_bf[:], tab[1, rows, :])
 
-            if r == 0:
-                nc.sync.dma_start(weights[:], w.rearrange("(r p) m -> p r m", p=P))
-                nc.sync.dma_start(bias[:], b.rearrange("(h p) one -> p (h one)", p=P))
-
-            gains = wide.tile([P, S], F32)
-            nc.scalar.copy(gains[:], gains_bf[:])
             features = wide.tile([P, N], F32)
             nc.scalar.copy(features[:], features_bf[:])
+            gains = wide.tile([P, S], F32)
+            if r == 0:
+                nc.vector.tensor_copy(gains[:], gains_bf[:])
+            else:
+                nc.scalar.copy(gains[:], gains_bf[:])
             shifts = wide.tile([P, S], F32)
             nc.scalar.copy(shifts[:], shifts_bf[:])
+            return features, gains, shifts
 
-            scaled = wide.tile([P, N], F32)
-            nc.vector.tensor_tensor(scaled[:], gains[:].indirect(offsets[:]), features[:], MULT)
+        block = load_and_widen(0)
+        nc.sync.dma_start(weights[:], w.rearrange("(r p) m -> p r m", p=P))
+        nc.sync.dma_start(bias[:], b.rearrange("(h p) one -> p (h one)", p=P))
 
-            for c in range(PIECES):
-                columns = slice(c * PIECE, (c + 1) * PIECE)
-                list_columns = slice(
-                    c * PIECE // OFFSETS_PER_COLUMN, (c + 1) * PIECE // OFFSETS_PER_COLUMN
-                )
-                x = pieces.tile([P, PIECE], F32)
-                nc.vector.tensor_tensor(
-                    x[:], shifts[:].indirect(offsets[:, list_columns]), scaled[:, columns], ADD
-                )
-                x_bf = pieces.tile([P, PIECE], BF16)
-                nc.scalar.copy(x_bf[:], x[:])
-                for h in range(HALVES):
-                    nc.tensor.matmul(
-                        sums[h][c][:],
-                        weights[:, r, h * P : (h + 1) * P],
-                        x_bf[:],
-                        start=(r == 0),
-                        stop=(r == BLOCKS - 1),
+        for r in range(BLOCKS):
+            features, gains, shifts = block
+            if r + 1 < BLOCKS:
+                block = load_and_widen(r + 1)
+
+            scaled_before = None
+            for step in range(PIECES + 1):
+                if step < PIECES:
+                    scaled = pieces.tile([P, PIECE], F32)
+                    nc.vector.tensor_tensor(
+                        scaled[:],
+                        gains[:].indirect(offsets[:, list_columns(step)]),
+                        features[:, columns(step)],
+                        MULT,
                     )
-
-        for c in range(PIECES):
-            columns = slice(c * PIECE, (c + 1) * PIECE)
-            for h in range(HALVES):
-                result = pieces.tile([P, PIECE], F32)
-                nc.scalar.activation(result[:], sums[h][c][:], RELU, bias=bias[:, h : h + 1])
-                nc.sync.dma_start(out[h * P : (h + 1) * P, columns], result[:])
+                if step > 0:
+                    c = step - 1
+                    x = pieces.tile([P, PIECE], F32)
+                    nc.vector.tensor_tensor(
+                        x[:], shifts[:].indirect(offsets[:, list_columns(c)]), scaled_before[:], ADD
+                    )
+                    x_bf = pieces.tile([P, PIECE], BF16)
+                    if r == BLOCKS - 1 and c == PIECES - 1:
+                        nc.vector.tensor_copy(x_bf[:], x[:])
+                    else:
+                        nc.scalar.copy(x_bf[:], x[:])
+                    for h in range(HALVES):
+                        nc.tensor.matmul(
+                            sums[h][c][:],
+                            weights[:, r, h * P : (h + 1) * P],
+                            x_bf[:],
+                            start=(r == 0),
+                            stop=(r == BLOCKS - 1),
+                        )
+                    if r == BLOCKS - 1:
+                        for h in range(HALVES):
+                            result = pieces.tile([P, PIECE], F32)
+                            if c == PIECES - 1 and h == HALVES - 1:
+                                nc.vector.tensor_scalar(
+                                    result[:], sums[h][c][:], bias[:, h : h + 1], 0.0, ADD, MAX
+                                )
+                            else:
+                                nc.scalar.activation(
+                                    result[:], sums[h][c][:], RELU, bias=bias[:, h : h + 1]
+                                )
+                            nc.sync.dma_start(out[h * P : (h + 1) * P, columns(c)], result[:])
+                scaled_before = scaled

@@ -46,20 +46,21 @@ def tile_lookup_film_mul_relu_kernel(tc, tab, x0, w, b, offs, out):
 
         def load_and_widen(r):
             rows = slice(r * P, (r + 1) * P)
-            features_bf = loaded.tile([P, N], BF16)
-            nc.sync.dma_start(features_bf[:], x0[rows, :])
             gains_bf = loaded.tile([P, S], BF16)
             nc.sync.dma_start(gains_bf[:], tab[0, rows, :])
+            features_bf = loaded.tile([P, N], BF16)
+            nc.sync.dma_start(features_bf[:], x0[rows, :])
             shifts_bf = loaded.tile([P, S], BF16)
             nc.sync.dma_start(shifts_bf[:], tab[1, rows, :])
 
-            features = wide.tile([P, N], F32)
-            nc.scalar.copy(features[:], features_bf[:])
             gains = wide.tile([P, S], F32)
             if r == 0:
                 nc.vector.tensor_copy(gains[:], gains_bf[:])
             else:
                 nc.scalar.copy(gains[:], gains_bf[:])
+            features = wide.tile([P, N], F32)
+            for c in range(PIECES):
+                nc.scalar.copy(features[:, columns(c)], features_bf[:, columns(c)])
             shifts = wide.tile([P, S], F32)
             nc.scalar.copy(shifts[:], shifts_bf[:])
             return features, gains, shifts
@@ -102,16 +103,15 @@ def tile_lookup_film_mul_relu_kernel(tc, tab, x0, w, b, offs, out):
                             start=(r == 0),
                             stop=(r == BLOCKS - 1),
                         )
-                    if r == BLOCKS - 1:
-                        for h in range(HALVES):
-                            result = pieces.tile([P, PIECE], F32)
-                            if c == PIECES - 1 and h == HALVES - 1:
-                                nc.vector.tensor_scalar(
-                                    result[:], sums[h][c][:], bias[:, h : h + 1], 0.0, ADD, MAX
-                                )
-                            else:
-                                nc.scalar.activation(
-                                    result[:], sums[h][c][:], RELU, bias=bias[:, h : h + 1]
-                                )
-                            nc.sync.dma_start(out[h * P : (h + 1) * P, columns(c)], result[:])
                 scaled_before = scaled
+
+        for c in range(PIECES):
+            for h in range(HALVES):
+                result = held.tile([P, PIECE], F32, name=f"result_{h}_{c}")
+                if c >= PIECES - 2 and h == HALVES - 1:
+                    nc.vector.tensor_scalar(
+                        result[:], sums[h][c][:], bias[:, h : h + 1], 0.0, ADD, MAX
+                    )
+                else:
+                    nc.scalar.activation(result[:], sums[h][c][:], RELU, bias=bias[:, h : h + 1])
+                nc.sync.dma_start(out[h * P : (h + 1) * P, columns(c)], result[:])

@@ -30,7 +30,7 @@ def tile_lookup_film_mul_relu_kernel(tc, tab, x0, w, b, offs, out):
         tc.tile_pool(name="held", bufs=1) as held,
         tc.tile_pool(name="loaded", bufs=2) as loaded,
         tc.tile_pool(name="wide", bufs=2) as wide,
-        tc.tile_pool(name="pieces", bufs=4) as pieces,
+        tc.tile_pool(name="pieces", bufs=PIECES + 1) as pieces,
         tc.psum_pool(name="psum", bufs=1) as psum,
     ):
         offsets = held.tile([P, N // OFFSETS_PER_COLUMN], U16)
@@ -44,20 +44,24 @@ def tile_lookup_film_mul_relu_kernel(tc, tab, x0, w, b, offs, out):
             for h in range(HALVES)
         ]
 
+        sides = [slice(0, S // 2), slice(S // 2, S)]
+
         def load_and_widen(r):
             rows = slice(r * P, (r + 1) * P)
             gains_bf = loaded.tile([P, S], BF16)
-            nc.sync.dma_start(gains_bf[:], tab[0, rows, :])
             features_bf = loaded.tile([P, N], BF16)
-            nc.sync.dma_start(features_bf[:], x0[rows, :])
+            for side in sides:
+                nc.sync.dma_start(gains_bf[:, side], tab[0, rows, side])
+                nc.sync.dma_start(features_bf[:, side], x0[rows, side])
             shifts_bf = loaded.tile([P, S], BF16)
             nc.sync.dma_start(shifts_bf[:], tab[1, rows, :])
 
             gains = wide.tile([P, S], F32)
-            if r == 0:
-                nc.vector.tensor_copy(gains[:], gains_bf[:])
-            else:
-                nc.scalar.copy(gains[:], gains_bf[:])
+            for side in sides:
+                if r == 0:
+                    nc.vector.tensor_copy(gains[:, side], gains_bf[:, side])
+                else:
+                    nc.scalar.copy(gains[:, side], gains_bf[:, side])
             features = wide.tile([P, N], F32)
             for c in range(PIECES):
                 nc.scalar.copy(features[:, columns(c)], features_bf[:, columns(c)])
@@ -74,21 +78,22 @@ def tile_lookup_film_mul_relu_kernel(tc, tab, x0, w, b, offs, out):
             if r + 1 < BLOCKS:
                 block = load_and_widen(r + 1)
 
-            scaled_before = None
-            for step in range(PIECES + 1):
+            lag = 1 if r == BLOCKS - 1 else PIECES
+            scaled = []
+            for step in range(PIECES + lag):
                 if step < PIECES:
-                    scaled = pieces.tile([P, PIECE], F32)
+                    scaled.append(pieces.tile([P, PIECE], F32, name="scaled"))
                     nc.vector.tensor_tensor(
-                        scaled[:],
+                        scaled[step][:],
                         gains[:].indirect(offsets[:, list_columns(step)]),
                         features[:, columns(step)],
                         MULT,
                     )
-                if step > 0:
-                    c = step - 1
+                if step >= lag:
+                    c = step - lag
                     x = pieces.tile([P, PIECE], F32)
                     nc.vector.tensor_tensor(
-                        x[:], shifts[:].indirect(offsets[:, list_columns(c)]), scaled_before[:], ADD
+                        x[:], shifts[:].indirect(offsets[:, list_columns(c)]), scaled[c][:], ADD
                     )
                     x_bf = pieces.tile([P, PIECE], BF16)
                     if r == BLOCKS - 1 and c == PIECES - 1:
@@ -103,7 +108,6 @@ def tile_lookup_film_mul_relu_kernel(tc, tab, x0, w, b, offs, out):
                             start=(r == 0),
                             stop=(r == BLOCKS - 1),
                         )
-                scaled_before = scaled
 
         for c in range(PIECES):
             for h in range(HALVES):

import concourse.mybir as mybir

BF16, F32, U16 = mybir.dt.bfloat16, mybir.dt.float32, mybir.dt.uint16
ADD, MAX, MULT = mybir.AluOpType.add, mybir.AluOpType.max, mybir.AluOpType.mult
RELU = mybir.ActivationFunctionType.Relu

P = 128
R, S, N, M = 512, 2048, 2048, 256
BLOCKS = R // P
HALVES = M // P
PIECE = 512
PIECES = N // PIECE
OFFSETS_PER_COLUMN = 16

FLOPS = 2 * R * N * M + 2 * R * N


def columns(c):
    return slice(c * PIECE, (c + 1) * PIECE)


def list_columns(c):
    width = PIECE // OFFSETS_PER_COLUMN
    return slice(c * width, (c + 1) * width)


def tile_lookup_film_mul_relu_kernel(tc, tab, x0, w, b, offs, out):
    nc = tc.nc
    with (
        tc.tile_pool(name="held", bufs=1) as held,
        tc.tile_pool(name="loaded", bufs=2) as loaded,
        tc.tile_pool(name="wide", bufs=2) as wide,
        tc.tile_pool(name="pieces", bufs=PIECES + 1) as pieces,
        tc.psum_pool(name="psum", bufs=1) as psum,
    ):
        offsets = held.tile([P, N // OFFSETS_PER_COLUMN], U16)
        nc.sync.dma_start(offsets[:], offs)

        weights = held.tile([P, BLOCKS, M], BF16)
        bias = held.tile([P, HALVES], F32)

        sums = [
            [psum.tile([P, PIECE], F32, name=f"sum_{h}_{c}") for c in range(PIECES)]
            for h in range(HALVES)
        ]

        sides = [slice(0, S // 2), slice(S // 2, S)]

        def load_and_widen(r):
            rows = slice(r * P, (r + 1) * P)
            gains_bf = loaded.tile([P, S], BF16)
            features_bf = loaded.tile([P, N], BF16)
            for side in sides:
                nc.sync.dma_start(gains_bf[:, side], tab[0, rows, side])
                nc.sync.dma_start(features_bf[:, side], x0[rows, side])
            shifts_bf = loaded.tile([P, S], BF16)
            nc.sync.dma_start(shifts_bf[:], tab[1, rows, :])

            gains = wide.tile([P, S], F32)
            for side in sides:
                if r == 0:
                    nc.vector.tensor_copy(gains[:, side], gains_bf[:, side])
                else:
                    nc.scalar.copy(gains[:, side], gains_bf[:, side])
            features = wide.tile([P, N], F32)
            for c in range(PIECES):
                nc.scalar.copy(features[:, columns(c)], features_bf[:, columns(c)])
            shifts = wide.tile([P, S], F32)
            nc.scalar.copy(shifts[:], shifts_bf[:])
            return features, gains, shifts

        block = load_and_widen(0)
        nc.sync.dma_start(weights[:], w.rearrange("(r p) m -> p r m", p=P))
        nc.sync.dma_start(bias[:], b.rearrange("(h p) one -> p (h one)", p=P))

        for r in range(BLOCKS):
            features, gains, shifts = block
            if r + 1 < BLOCKS:
                block = load_and_widen(r + 1)

            lag = 1 if r == BLOCKS - 1 else PIECES
            scaled = []
            for step in range(PIECES + lag):
                if step < PIECES:
                    scaled.append(pieces.tile([P, PIECE], F32, name="scaled"))
                    nc.vector.tensor_tensor(
                        scaled[step][:],
                        gains[:].indirect(offsets[:, list_columns(step)]),
                        features[:, columns(step)],
                        MULT,
                    )
                if step >= lag:
                    c = step - lag
                    x = pieces.tile([P, PIECE], F32)
                    nc.vector.tensor_tensor(
                        x[:], shifts[:].indirect(offsets[:, list_columns(c)]), scaled[c][:], ADD
                    )
                    x_bf = pieces.tile([P, PIECE], BF16)
                    if r == BLOCKS - 1 and c == PIECES - 1:
                        nc.vector.tensor_copy(x_bf[:], x[:])
                    else:
                        nc.scalar.copy(x_bf[:], x[:])
                    for h in range(HALVES):
                        nc.tensor.matmul(
                            sums[h][c][:],
                            weights[:, r, h * P : (h + 1) * P],
                            x_bf[:],
                            start=(r == 0),
                            stop=(r == BLOCKS - 1),
                        )

        for c in range(PIECES):
            for h in range(HALVES):
                result = held.tile([P, PIECE], F32, name=f"result_{h}_{c}")
                if c >= PIECES - 2 and h == HALVES - 1:
                    nc.vector.tensor_scalar(
                        result[:], sums[h][c][:], bias[:, h : h + 1], 0.0, ADD, MAX
                    )
                else:
                    nc.scalar.activation(result[:], sums[h][c][:], RELU, bias=bias[:, h : h + 1])
                nc.sync.dma_start(out[h * P : (h + 1) * P, columns(c)], result[:])
